import numpy as np
import ml_dtypes


def mxq(x, axis, fmt="e4m3"):
    dtype, down = {"e4m3": (ml_dtypes.float8_e4m3fn, 7), "e5m2": (ml_dtypes.float8_e5m2, 14)}[fmt]
    v = np.moveaxis(np.asarray(x, np.float32).astype(ml_dtypes.bfloat16).astype(np.float64), axis, -1)
    blocks = v.reshape(v.shape[:-1] + (-1, 32))
    amax = np.abs(blocks).max(-1, keepdims=True)
    byte = np.maximum(np.where(amax > 0, np.frexp(amax)[1] - 1 + 127, 0) - down, 1)
    scale = np.exp2(byte - 127.0)
    codes = (blocks / scale).astype(np.float32).astype(dtype).astype(np.float64)
    return np.moveaxis((codes * scale).reshape(v.shape), -1, axis)


WIDE = False


def mx_kscale(k):
    if not WIDE:
        return np.ones(k)
    levels = np.array([10, -10, 5, -5, 0])
    if k % 512:
        return np.exp2(np.random.permutation(np.resize(levels, k // 32))).repeat(32)
    a = np.empty((k // 512, 16))
    for p in range(k // 512):
        a[p, :8] = np.random.permutation(np.resize(levels, 8))
        for g in range(8):
            far = levels[np.abs(levels - a[p, g]) >= 10]
            a[p, g + 8] = far[np.random.randint(len(far))]
    return np.exp2(a.ravel()).repeat(32)


def f64(x):
    return np.asarray(x).astype(np.float64)


def striped(idx):
    return np.tile(np.asarray(idx).reshape(-1, 16).T, (8, 1)).astype(np.uint16)


def unstriped(offs):
    return offs[:16].T.reshape(-1).astype(np.int64)


E2M1 = np.array([0.0, 0.5, 1.0, 1.5, 2.0, 3.0, 4.0, 6.0, -0.0, -0.5, -1.0, -1.5, -2.0, -3.0, -4.0, -6.0])


def pack_weight(w, fmt):
    k, n = w.shape
    w = f64(np.asarray(w, np.float32).astype(ml_dtypes.bfloat16)).reshape(k // 32, 32, n)
    amax = np.abs(w).max(1)
    if fmt == "e4m3":
        byte = np.frexp(amax)[1] - 1 + 127 - 7
    else:
        mant, ex = np.frexp(amax / 6.0)
        byte = np.where(mant > 0.5, ex, ex - 1) + 127
    byte = np.clip(np.where(amax > 0, byte, 1), 1, 254)
    scaled = (w * np.exp2(127.0 - byte)[:, None, :]).reshape(k, n).astype(np.float32)
    by_word = np.ascontiguousarray(scaled.reshape(k // 512, 128, 4, n).transpose(0, 1, 3, 2))
    if fmt == "e4m3":
        words = by_word.astype(ml_dtypes.float8_e4m3fn).view(np.uint8)
    else:
        c = by_word.astype(ml_dtypes.float4_e2m1fn).view(np.uint8) & 0xF
        words = (c[..., 0::2] | (c[..., 1::2] << 4)).reshape(k // 512, 128, 2 * n)
    return np.ascontiguousarray(words), np.ascontiguousarray(byte.astype(np.uint8).reshape(k // 512, 16, n))


def unpack_weight(words, scales, fmt):
    g, _, n = scales.shape
    words = np.ascontiguousarray(words).reshape(g, 128, n, -1)
    if fmt == "e4m3":
        vals = words.view(ml_dtypes.float8_e4m3fn).astype(np.float64)
    else:
        nib = np.empty((g, 128, n, 4), np.uint8)
        nib[..., 0::2] = words & 0xF
        nib[..., 1::2] = words >> 4
        vals = E2M1[nib]
    vals = vals * np.repeat(np.exp2(scales.astype(np.float64) - 127.0), 8, axis=1)[..., None]
    return vals.transpose(0, 1, 3, 2).reshape(g * 512, n)


D, T, I, Q, E, Z, M = 512, 2048, 512, 256, 512, 1024, 1024


def setup_inputs():
    n = np.random.standard_normal
    idx = np.random.permutation(T)[:I]
    idx2 = np.random.permutation(Z)[:I]
    idx3 = np.random.permutation(M)[:Q]
    fd = mx_kscale(D)
    fi = mx_kscale(I)
    ti = np.ones(T)
    ti[idx] = fi
    keysp = pack_weight(n((D, T)) / fd[:, None], "e4m3")
    return {
        "query": (n((D, Q)) * 1.0 / np.sqrt(D) * fd[:, None]).astype(np.float32),
        "query2": (n((D, Q)) * 1.0 / np.sqrt(D) * fd[:, None]).astype(np.float32),
        "keys_words": keysp[0],
        "keys_scales": keysp[1],
        "pages": (n((D, Z)) / fd[:, None]).astype(np.float32),
        "os": (np.random.uniform(0.02, 0.08, (1, I)) * fi).astype(np.float32),
        "vals": (n((E, T)) / ti).astype(np.float32),
        "old": (n((E, M)) * 2.0).astype(np.float32),
        "fade": (np.random.uniform(0.3, 0.9, (1, M))).astype(np.float32),
        "offs": striped(idx),
        "offs2": striped(idx2),
        "offs3": striped(idx3),
    }


def reference(query, query2, keys_words, keys_scales, pages, os, vals, old, fade, offs, offs2, offs3):
    idx = unstriped(offs)
    idx2 = unstriped(offs2)
    idx3 = unstriped(offs3)
    keysu = unpack_weight(keys_words, keys_scales, "e4m3")
    queryq = mxq(f64(query), 0, "e4m3")
    keysidxg = keysu[:, idx]
    a = queryq.T @ keysidxg
    query2q = mxq(f64(query2), 0, "e4m3")
    pagesq = mxq(f64(pages), 0, "e4m3")
    h0 = query2q.T @ pagesq
    s = np.maximum(a, h0[:, idx2])
    w = np.maximum(s, 0.0)
    wo1 = w * f64(os)
    wt1 = wo1.T
    vt1 = f64(vals)[:, idx].T
    vt1q = mxq(vt1, 0, "e4m3")
    wt1q = mxq(wt1, 0, "e4m3")
    o = vt1q.T @ wt1q
    of = np.zeros((E, M))
    of[:, idx3] = o
    y = f64(old) * f64(fade) + of
    return y

@@ -1,0 +1,250 @@
+from contextlib import ExitStack
+
+import concourse.mybir as mybir
+from concourse.masks import make_identity
+
+D, T, I, Q, E, Z, M = 512, 2048, 512, 256, 512, 1024, 1024
+FLOPS = 2 * D * Q * I + 2 * D * Q * Z + 2 * I * E * Q
+
+F32 = mybir.dt.float32
+BF16 = mybir.dt.bfloat16
+I32 = mybir.dt.int32
+U32 = mybir.dt.uint32
+U16 = mybir.dt.uint16
+U8 = mybir.dt.uint8
+FP8X4 = mybir.dt.float8_e4m3fn_x4
+COPY = mybir.ActivationFunctionType.Copy
+MAX = mybir.AluOpType.max
+MULT = mybir.AluOpType.mult
+ADD = mybir.AluOpType.add
+
+P = 128
+PACK = 4
+BANK = 512
+Q_TILES = Q // P
+E_TILES = E // P
+Z_HALVES = Z // BANK
+FADE_RUN = M // P
+LOADS = ["l1","q2","fade","kb","p0","p1","kw","q","l2","slot","l3","v0","v1","v2","o0","v3","o1","o2","o3"]
+STEPS = ["ilq2","gkb","qzq2","fade","ip0","qp0","ip1","qp1","ch00","ch01","ch10","ch11","gkw","ilq","qzq","gh0","gh1","gv0","mx1","mx0","mw1","mw0","cv0","gv1","qzw","qv0","gv2","cv1","co0","mu0","qv1","sc0","cv2","co1","gv3","qv2","sc1","ad0","cv3","mu1","co2","qv3","sc2","ad1","mu2","co3","sc3","ad2","mu3","ad3h"]
+ON_SCALAR = ["ips","ch00","ch01","ch10","ch11","gh0","gv0","gv1","cv0","cv1","cv2","cv3","co0","co1","co2","co3","sc0","sc1","sc2","sc3"]
+PLACES = {"vals3":0,"sum0":0,"vals2_codes":4096,"old0":8192,"vals1_codes":8192,"old1":12288,"vals3_codes":12288,"picked_vals1":16384,"result0":16384,"picked_vals2":17408,"result1":17408,"picked_vals3":18432,"result2":18432}
+BANKS = {"f0":0,"f1":1,"ch00":2,"ch01":3,"ch10":0,"ch11":1,"mx1":2,"mx0":3,"mw1":0,"mw0":1,"cv0":3,"cv1":4,"cv2":5,"cv3":4,"co0":6,"co1":7,"co2":6,"co3":7}
+PAGES_ON_VECTOR = 320
+
+
+def tile_attend_widelarger_written_lean_kernel(
+    tc, query, query2, keys_words, keys_scales, pages, slot_scale, vals, old, fade, offs, offs2, offs3, out
+):
+    nc = tc.nc
+
+    with ExitStack() as ctx:
+        sb = ctx.enter_context(tc.tile_pool(name="sb", bufs=1))
+        shared = ctx.enter_context(tc.tile_pool(name="shared", bufs=1))
+        ps = ctx.enter_context(tc.psum_pool(name="ps", bufs=1))
+
+        def bank(name, shape):
+            return ps.tile(shape, F32, name=name, tag="bank%d" % BANKS[name])
+
+        def new(name, shape, dtype, align=32):
+            if name in PLACES:
+                return shared.tile(shape, dtype, name=name, offset=PLACES[name], align_bytes=64)
+            return sb.tile(shape, dtype, name=name, align_bytes=64)
+
+        def load_rows(name, rows):
+            raw = new(name, [P, PACK, rows.shape[1]], F32)
+            nc.sync.dma_start(out=raw[:], in_=rows.rearrange("(p j) w -> p j w", j=PACK))
+            return raw
+
+        def load_plain(name, src, dtype):
+            t = new(name, [P, src.shape[1]], dtype)
+            nc.sync.dma_start(out=t[:], in_=src)
+            return t
+
+        def copy_on(step, dst, src):
+            if step in ON_SCALAR:
+                nc.scalar.copy(out=dst, in_=src)
+            else:
+                nc.vector.tensor_copy(out=dst, in_=src)
+
+        def interleave(step, grouped, raw, cols):
+            dst = grouped[:, cols, :].rearrange("p (c i) j -> p c j i", i=4)
+            src = raw[:, :, cols].rearrange("p j (c i) -> p c j i", i=4)
+            copy_on(step, dst, src)
+
+        def quantise(name, grouped):
+            width = grouped.shape[1]
+            codes = new(name + "_codes", [P, width], U32)
+            scales = new(name + "_scales", [P, width], U8)
+            nc.vector.quantize_mx(
+                out=codes[:].bitcast(FP8X4), scales=scales[:], in_=grouped[:].rearrange("p w j -> p (w j)")
+            )
+            return codes, scales
+
+        def product(acc, stat, stat_cols, mov):
+            nc.tensor.matmul_mx(
+                out=acc,
+                lhsT=stat[0][:, stat_cols].bitcast(FP8X4),
+                lhsT_scale=stat[1][:, stat_cols],
+                rhs=mov[0][:].bitcast(FP8X4),
+                rhs_scale=mov[1][:],
+                start=True,
+                stop=True,
+            )
+
+        def listed(step, dst, src):
+            if step in ON_SCALAR:
+                nc.scalar.activation(out=dst, in_=src, func=COPY)
+            else:
+                nc.vector.tensor_copy(out=dst, in_=src)
+
+        def probe(name, src):
+            t = new(name, [P, src.shape[1]], src.dtype)
+            nc.gpsimd.tensor_copy(out=t[:], in_=src)
+
+        key_bytes = new("key_bytes", [P, T], U8)
+        nc.gpsimd.memset(key_bytes[:].bitcast(I32), 0)
+        placed = []
+        for c in range(E_TILES):
+            window = new("placed%d" % c, [P, M], F32)
+            nc.vector.memset(window[:], 0.0)
+            placed.append(window)
+        identity = new("identity", [P, P], F32)
+        make_identity(nc, identity[:])
+
+        t = {}
+        for name in LOADS:
+            if name == "q2":
+                t[name] = load_rows("q2_raw", query2)
+            elif name == "q":
+                t[name] = load_rows("q_raw", query)
+            elif name in ("p0", "p1"):
+                h = int(name[1])
+                t[name] = load_rows("pages_raw%d" % h, pages[:, h * BANK : (h + 1) * BANK])
+            elif name == "fade":
+                t[name] = load_plain("fade_runs", fade.rearrange("o (n c) -> (o n) c", c=FADE_RUN), F32)
+            elif name == "slot":
+                t[name] = load_plain("slot_factor", slot_scale.rearrange("o (p t) -> (o p) t", t=PACK), F32)
+            elif name == "l1":
+                t[name] = load_plain("token_list", offs, U16)
+            elif name == "l2":
+                t[name] = load_plain("page_list", offs2, U16)
+            elif name == "l3":
+                t[name] = load_plain("column_list", offs3, U16)
+            elif name == "kb":
+                for quad in range(4):
+                    nc.sync.dma_start(
+                        out=key_bytes[32 * quad : 32 * quad + 4, :].bitcast(I32),
+                        in_=keys_scales[0, 4 * quad : 4 * quad + 4, :].bitcast(I32),
+                    )
+            elif name == "kw":
+                t[name] = new("key_words", [P, T], U32)
+                nc.sync.dma_start(
+                    out=t[name][:].bitcast(I32), in_=keys_words[0].rearrange("p n t -> p (n t)").bitcast(I32)
+                )
+            elif name[0] == "v":
+                c = int(name[1])
+                t[name] = load_plain("vals%d" % c, vals[c * P : (c + 1) * P, :], F32)
+            else:
+                c = int(name[1])
+                t[name] = load_plain("old%d" % c, old[c * P : (c + 1) * P, :], F32)
+
+        fade_sb = new("fade_sb", [P, P, FADE_RUN], F32)
+        fade_row = fade_sb[:].rearrange("p n c -> p (n c)")
+        h0 = [new("h0_%d" % r, [P, Z], F32) for r in range(Q_TILES)]
+        w_grouped = new("w_grouped", [P, Q, PACK], BF16)
+
+        for step in STEPS:
+            kind, c = step[:2], step[2:3]
+            if step in ("ilq", "ilq2"):
+                name = step[2:]
+                t["g" + name] = new(name + "_grouped", [P, Q, PACK], BF16)
+                interleave(step, t["g" + name], t[name], slice(0, Q))
+            elif step in ("qzq", "qzq2"):
+                t["m" + step[2:]] = quantise(step[2:], t["g" + step[2:]])
+            elif step == "fade":
+                for h in range(FADE_RUN // 4):
+                    spread = bank("f%d" % h, [P, 4, P])
+                    for j in range(4):
+                        k = 4 * h + j
+                        nc.tensor.transpose(spread[:, j, :], t["fade"][:, k : k + 1].to_broadcast([P, P]), identity[:])
+                    nc.scalar.copy(out=fade_sb[:, :, 4 * h : 4 * h + 4], in_=spread[:].rearrange("p c n -> p n c"))
+            elif kind == "ip":
+                t["gp" + c] = new("pages_grouped" + c, [P, BANK, PACK], BF16)
+                interleave("ipv", t["gp" + c], t["p" + c], slice(0, PAGES_ON_VECTOR))
+                interleave("ips", t["gp" + c], t["p" + c], slice(PAGES_ON_VECTOR, BANK))
+            elif kind == "qp":
+                t["mp" + c] = quantise("pages" + c, t["gp" + c])
+            elif kind == "ch":
+                h, r = int(step[2]), int(step[3])
+                acc = bank(step, [P, BANK])
+                product(acc[:], t["mq2"], slice(r * P, (r + 1) * P), t["mp" + c])
+                copy_on(step, h0[r][:, h * BANK : (h + 1) * BANK], acc[:])
+            elif kind == "gh":
+                t[step] = new("page_score" + c, [P, I], F32)
+                listed(step, t[step][:], h0[int(c)][:].indirect(t["l2"][:]))
+            elif step == "gkb":
+                t[step] = new("picked_bytes", [P, I], U8)
+                listed(step, t[step][:], key_bytes[:].indirect(t["l1"][:]))
+            elif step == "gkw":
+                t[step] = new("picked_words", [P, I], U32)
+                listed(step, t[step][:], t["kw"][:].indirect(t["l1"][:]))
+            elif kind == "mx":
+                r = int(c)
+                acc = bank(step, [P, I])
+                product(acc[:], t["mq"], slice(r * P, (r + 1) * P), (t["gkw"], t["gkb"]))
+                t[step] = new("score" + c, [P, PACK, P], F32)
+                nc.vector.tensor_tensor(
+                    out=t[step][:].rearrange("q t (a i) -> q a t i", i=4),
+                    in0=acc[:].rearrange("q (a i t) -> q a t i", i=4, t=PACK),
+                    in1=t["gh" + c][:].rearrange("q (a i t) -> q a t i", i=4, t=PACK),
+                    op=MAX,
+                )
+            elif kind == "mw":
+                r = int(c)
+                turned_w = bank(step, [P, PACK, P])
+                for j in range(PACK):
+                    nc.tensor.transpose(turned_w[:, j, :], t["mx" + c][:, j, :], identity[:])
+                nc.vector.scalar_tensor_tensor(
+                    out=w_grouped[:, r * P : (r + 1) * P, :],
+                    in0=turned_w[:].rearrange("p t q -> p q t"),
+                    scalar=0.0,
+                    in1=t["slot"][:].unsqueeze(1).to_broadcast([P, P, PACK]),
+                    op0=MAX,
+                    op1=MULT,
+                )
+            elif step == "qzw":
+                t["mw"] = quantise("w", w_grouped)
+            elif kind == "gv":
+                t[step] = new("picked_vals" + c, [P, I], BF16)
+                listed(step, t[step][:], t["v" + c][:].indirect(t["l1"][:]))
+            elif kind == "cv":
+                pairs = t["gv" + c][:].bitcast(F32)
+                turned = bank(step, [P, 2, P])
+                for u in range(2):
+                    nc.tensor.transpose(turned[:, u, :], pairs[:, u : I // 2 : 2], identity[:])
+                t[step] = new("vals_grouped" + c, [P, P, PACK], BF16)
+                copy_on(step, t[step][:].bitcast(F32), turned[:].rearrange("p u e -> p e u"))
+            elif kind == "qv":
+                t[step] = quantise("vals" + c, t["cv" + c])
+            elif kind == "co":
+                acc = bank(step, [P, Q])
+                product(acc[:], t["qv" + c], slice(0, P), t["mw"])
+                t[step] = new("result" + c, [P, Q], F32)
+                copy_on(step, t[step][:], acc[:])
+            elif kind == "sc":
+                listed(step, placed[int(c)][:].indirect(t["l3"][:]), t["co" + c][:])
+            elif kind == "mu":
+                t[step] = new("faded" + c, [P, M], F32)
+                nc.vector.tensor_tensor(out=t[step][:], in0=t["o" + c][:], in1=fade_row, op=MULT)
+            elif kind == "ad":
+                pieces = 2 if len(step) == 4 else 1
+                y = new("sum" + c, [P, M], F32)
+                for k in range(pieces):
+                    cols = slice(k * M // pieces, (k + 1) * M // pieces)
+                    nc.vector.tensor_tensor(out=y[:, cols], in0=t["mu" + c][:, cols], in1=placed[int(c)][:, cols], op=ADD)
+                    nc.sync.dma_start(out=out[int(c) * P : (int(c) + 1) * P, cols], in_=y[:, cols])
+            elif step == "probe1":
+                probe(step, t["co0"][:, 0:1])
+            elif step == "probe2":
+                probe(step, t["co3"][:, 0:1])

@@ -25,12 +25,13 @@ Q_TILES = Q // P
 E_TILES = E // P
 Z_HALVES = Z // BANK
 FADE_RUN = M // P
-LOADS = ["l1","q2","fade","kb","p0","p1","kw","q","l2","slot","l3","v0","v1","v2","o0","v3","o1","o2","o3"]
-STEPS = ["ilq2","gkb","qzq2","fade","ip0","qp0","ip1","qp1","ch00","ch01","ch10","ch11","gkw","ilq","qzq","gh0","gh1","gv0","mx1","mx0","mw1","mw0","cv0","gv1","qzw","qv0","gv2","cv1","co0","mu0","qv1","sc0","cv2","co1","gv3","qv2","sc1","ad0","cv3","mu1","co2","qv3","sc2","ad1","mu2","co3","sc3","ad2","mu3","ad3h"]
+LOADS = ["l1","q2","l2","kb","p0","p1","kw","q","slot","fade","l3","v0","v1","v2","o0","v3","o1","o2","o3"]
+STEPS = ["ilq2","gkb","qzq2","ip0","qp0","ip1","qp1","ch00","ch01","ch10","ch11","gkw","ilq","qzq","gh0","gh1","gv0","mx1","mx0","mw1","mw0","fade","cv0","gv1","qzw","qv0","gv2","cv1","co0","mu0","qv1","sc0","cv2","co1","gv3","qv2","sc1","ad0h","cv3","mu1","co2","qv3","sc2","ad1h","mu2","co3","sc3","mu3","ad2h","ad3h"]
 ON_SCALAR = ["ips","ch00","ch01","ch10","ch11","gh0","gv0","gv1","cv0","cv1","cv2","cv3","co0","co1","co2","co3","sc0","sc1","sc2","sc3"]
-PLACES = {"vals3":0,"sum0":0,"vals2_codes":4096,"old0":8192,"vals1_codes":8192,"old1":12288,"vals3_codes":12288,"picked_vals1":16384,"result0":16384,"picked_vals2":17408,"result1":17408,"picked_vals3":18432,"result2":18432}
-BANKS = {"f0":0,"f1":1,"ch00":2,"ch01":3,"ch10":0,"ch11":1,"mx1":2,"mx0":3,"mw1":0,"mw0":1,"cv0":3,"cv1":4,"cv2":5,"cv3":4,"co0":6,"co1":7,"co2":6,"co3":7}
+PLACES = {"vals3":0,"vals2_codes":0,"old0":8192,"vals1_codes":8192,"old1":12288,"vals3_codes":12288,"picked_vals1":16384,"result0":16384,"picked_vals2":17408,"result1":17408,"picked_vals3":18432,"result2":18432,"old3":20480,"sum2":20480}
+BANKS = {"ch00":0,"ch01":1,"ch10":2,"ch11":3,"mx1":4,"mx0":5,"mw1":6,"mw0":7,"f0":6,"f1":7,"cv0":5,"cv1":4,"cv2":5,"cv3":4,"co0":0,"co1":1,"co2":2,"co3":3}
 PAGES_ON_VECTOR = 320
+ON_GPSIMD = ["ad0a","ad0b","ad1a","ad1b"]
 
 
 def tile_attend_widelarger_written_lean_kernel(
@@ -122,7 +123,8 @@ def tile_attend_widelarger_written_lean_kernel(
                 h = int(name[1])
                 t[name] = load_rows("pages_raw%d" % h, pages[:, h * BANK : (h + 1) * BANK])
             elif name == "fade":
-                t[name] = load_plain("fade_runs", fade.rearrange("o (n c) -> (o n) c", c=FADE_RUN), F32)
+                t[name] = new("fade_runs", [P, 2, 4], F32)
+                nc.sync.dma_start(out=t[name][:], in_=fade.rearrange("o (h n c) -> n (o h) c", h=2, c=4))
             elif name == "slot":
                 t[name] = load_plain("slot_factor", slot_scale.rearrange("o (p t) -> (o p) t", t=PACK), F32)
             elif name == "l1":
@@ -149,8 +151,7 @@ def tile_attend_widelarger_written_lean_kernel(
                 c = int(name[1])
                 t[name] = load_plain("old%d" % c, old[c * P : (c + 1) * P, :], F32)
 
-        fade_sb = new("fade_sb", [P, P, FADE_RUN], F32)
-        fade_row = fade_sb[:].rearrange("p n c -> p (n c)")
+        fade_ps = []
         h0 = [new("h0_%d" % r, [P, Z], F32) for r in range(Q_TILES)]
         w_grouped = new("w_grouped", [P, Q, PACK], BF16)
 
@@ -166,9 +167,8 @@ def tile_attend_widelarger_written_lean_kernel(
                 for h in range(FADE_RUN // 4):
                     spread = bank("f%d" % h, [P, 4, P])
                     for j in range(4):
-                        k = 4 * h + j
-                        nc.tensor.transpose(spread[:, j, :], t["fade"][:, k : k + 1].to_broadcast([P, P]), identity[:])
-                    nc.scalar.copy(out=fade_sb[:, :, 4 * h : 4 * h + 4], in_=spread[:].rearrange("p c n -> p n c"))
+                        nc.tensor.transpose(spread[:, j, :], t["fade"][:, h, j : j + 1].to_broadcast([P, P]), identity[:])
+                    fade_ps.append(spread)
             elif kind == "ip":
                 t["gp" + c] = new("pages_grouped" + c, [P, BANK, PACK], BF16)
                 interleave("ipv", t["gp" + c], t["p" + c], slice(0, PAGES_ON_VECTOR))
@@ -236,13 +236,21 @@ def tile_attend_widelarger_written_lean_kernel(
                 listed(step, placed[int(c)][:].indirect(t["l3"][:]), t["co" + c][:])
             elif kind == "mu":
                 t[step] = new("faded" + c, [P, M], F32)
-                nc.vector.tensor_tensor(out=t[step][:], in0=t["o" + c][:], in1=fade_row, op=MULT)
+                for h in range(2):
+                    cols = slice(h * BANK, (h + 1) * BANK)
+                    nc.vector.tensor_tensor(
+                        out=t[step][:, cols].rearrange("p (n c) -> p n c", c=4),
+                        in0=t["o" + c][:, cols].rearrange("p (n c) -> p n c", c=4),
+                        in1=fade_ps[h][:].rearrange("p c n -> p n c"),
+                        op=MULT,
+                    )
             elif kind == "ad":
                 pieces = 2 if len(step) == 4 else 1
                 y = new("sum" + c, [P, M], F32)
                 for k in range(pieces):
                     cols = slice(k * M // pieces, (k + 1) * M // pieces)
-                    nc.vector.tensor_tensor(out=y[:, cols], in0=t["mu" + c][:, cols], in1=placed[int(c)][:, cols], op=ADD)
+                    adder = nc.gpsimd if step[:3] + "ab"[k] in ON_GPSIMD else nc.vector
+                    adder.tensor_tensor(out=y[:, cols], in0=t["mu" + c][:, cols], in1=placed[int(c)][:, cols], op=ADD)
                     nc.sync.dma_start(out=out[int(c) * P : (int(c) + 1) * P, cols], in_=y[:, cols])
             elif step == "probe1":
                 probe(step, t["co0"][:, 0:1])

@@ -25,11 +25,11 @@ Q_TILES = Q // P
 E_TILES = E // P
 Z_HALVES = Z // BANK
 FADE_RUN = M // P
-LOADS = ["l1","q2","l2","kb","p0","p1","kw","q","slot","fade","l3","v0","v1","v2","o0","v3","o1","o2","o3"]
-STEPS = ["ilq2","gkb","qzq2","ip0","qp0","ip1","qp1","ch00","ch01","ch10","ch11","gkw","ilq","qzq","gh0","gh1","gv0","mx1","mx0","mw1","mw0","fade","cv0","gv1","qzw","qv0","gv2","cv1","co0","mu0","qv1","sc0","cv2","co1","gv3","qv2","sc1","ad0h","cv3","mu1","co2","qv3","sc2","ad1h","mu2","co3","sc3","mu3","ad2h","ad3h"]
+LOADS = ["l1","q2","fade","kb","p0","p1","kw","q","l2","slot","l3","v0","v1","v2","o0","v3","o1","o2","o3"]
+STEPS = ["ilq2","gkb","qzq2","fade","ip0","qp0","ip1","qp1","ch00","ch01","ch10","ch11","gkw","ilq","qzq","gh0","gh1","gv0","mx1","mx0","mw1","mw0","cv0","gv1","qzw","qv0","gv2","cv1","co0","mu0","qv1","sc0","cv2","co1","gv3","qv2","sc1","ad0h","cv3","mu1","co2","qv3","sc2","ad1h","mu2","co3","sc3","mu3","ad2h","ad3h"]
 ON_SCALAR = ["ips","ch00","ch01","ch10","ch11","gh0","gv0","gv1","cv0","cv1","cv2","cv3","co0","co1","co2","co3","sc0","sc1","sc2","sc3"]
-PLACES = {"vals3":0,"vals2_codes":0,"old0":8192,"vals1_codes":8192,"old1":12288,"vals3_codes":12288,"picked_vals1":16384,"result0":16384,"picked_vals2":17408,"result1":17408,"picked_vals3":18432,"result2":18432,"old3":20480,"sum2":20480}
-BANKS = {"ch00":0,"ch01":1,"ch10":2,"ch11":3,"mx1":4,"mx0":5,"mw1":6,"mw0":7,"f0":6,"f1":7,"cv0":5,"cv1":4,"cv2":5,"cv3":4,"co0":0,"co1":1,"co2":2,"co3":3}
+PLACES = {"vals3":0,"vals2_codes":0,"old0":8192,"vals1_codes":8192,"old1":12288,"vals3_codes":12288,"picked_vals1":16384,"result0":16384,"picked_vals2":17408,"result1":17408,"picked_vals3":18432,"result2":18432,"old3":20480,"sum2":20480,"faded2":24576,"sum3":24576}
+BANKS = {"ch00":0,"ch01":1,"ch10":2,"ch11":3,"mx1":4,"mx0":5,"mw1":0,"mw0":1,"f0":6,"f1":7,"cv0":5,"cv1":4,"cv2":5,"cv3":4,"co0":2,"co1":3,"co2":0,"co3":1}
 PAGES_ON_VECTOR = 320
 ON_GPSIMD = ["ad0a","ad0b","ad1a","ad1b"]
 
@@ -253,6 +253,6 @@ def tile_attend_widelarger_written_lean_kernel(
                     adder.tensor_tensor(out=y[:, cols], in0=t["mu" + c][:, cols], in1=placed[int(c)][:, cols], op=ADD)
                     nc.sync.dma_start(out=out[int(c) * P : (int(c) + 1) * P, cols], in_=y[:, cols])
             elif step == "probe1":
-                probe(step, t["co0"][:, 0:1])
+                probe(step, w_grouped[:, Q - 1 : Q, 0])
             elif step == "probe2":
                 probe(step, t["co3"][:, 0:1])

@@ -25,13 +25,13 @@ Q_TILES = Q // P
 E_TILES = E // P
 Z_HALVES = Z // BANK
 FADE_RUN = M // P
-LOADS = ["l1","q2","fade","kb","p0","p1","kw","q","l2","slot","l3","v0","v1","v2","o0","v3","o1","o2","o3"]
-STEPS = ["ilq2","gkb","qzq2","fade","ip0","qp0","ip1","qp1","ch00","ch01","ch10","ch11","gkw","ilq","qzq","gh0","gh1","gv0","mx1","mx0","mw1","mw0","cv0","gv1","qzw","qv0","gv2","cv1","co0","mu0","qv1","sc0","cv2","co1","gv3","qv2","sc1","ad0h","cv3","mu1","co2","qv3","sc2","ad1h","mu2","co3","sc3","mu3","ad2h","ad3h"]
+LOADS = ["q2","l1","fade","kb","p0","p1","q","kw","l2","v0","slot","v1","l3","v2","o0","v3","o1","o2","o3"]
+STEPS = ["ilq2","gkb","qzq2","fade","ip0","qp0","ip1","qp1","ch00","ch01","ch10","ch11","ilq","qzq","gkw","gh0","gh1","gv0","mx0","mx1","mw0","mw1","cv0","gv1","qzw","qv0","gv2","cv1","co0","mu0","qv1","sc0","cv2","co1","gv3","qv2","sc1","cv3","mu1","co2","ad0h","qv3","sc2","mu2","co3","sc3","mu3","ad1h","ad2h","ad3q"]
 ON_SCALAR = ["ips","ch00","ch01","ch10","ch11","gh0","gv0","gv1","cv0","cv1","cv2","cv3","co0","co1","co2","co3","sc0","sc1","sc2","sc3"]
-PLACES = {"vals3":0,"vals2_codes":0,"old0":8192,"vals1_codes":8192,"old1":12288,"vals3_codes":12288,"picked_vals1":16384,"result0":16384,"picked_vals2":17408,"result1":17408,"picked_vals3":18432,"result2":18432,"old3":20480,"sum2":20480,"faded2":24576,"sum3":24576}
-BANKS = {"ch00":0,"ch01":1,"ch10":2,"ch11":3,"mx1":4,"mx0":5,"mw1":0,"mw0":1,"f0":6,"f1":7,"cv0":5,"cv1":4,"cv2":5,"cv3":4,"co0":2,"co1":3,"co2":0,"co3":1}
+PLACES = {"vals3":0,"vals2_codes":0,"old0":8192,"vals1_codes":8192,"old1":12288,"vals3_codes":12288,"sum0b":14336,"picked_vals1":16384,"result0":16384,"picked_vals2":17408,"result1":17408,"picked_vals3":18432,"result2":18432,"vals_grouped2":19456,"sum0a":19456,"sum1":21504,"vals_grouped3":25088,"faded2":25600,"sum3":25600,"old2":31744,"faded3":31744,"old3":35840,"sum2":35840,"pages_grouped1":44032,"q_grouped":44032,"picked_words":44032}
+BANKS = {"ch00":0,"ch01":1,"ch10":2,"ch11":3,"mx1":5,"mx0":4,"mw1":1,"mw0":0,"f0":6,"f1":7,"cv0":5,"cv1":4,"cv2":5,"cv3":4,"co0":2,"co1":3,"co2":0,"co3":1}
 PAGES_ON_VECTOR = 320
-ON_GPSIMD = ["ad0a","ad0b","ad1a","ad1b"]
+ON_GPSIMD = ["ad0a","ad1a","ad1b"]
 
 
 def tile_attend_widelarger_written_lean_kernel(
@@ -245,13 +245,15 @@ def tile_attend_widelarger_written_lean_kernel(
                         op=MULT,
                     )
             elif kind == "ad":
-                pieces = 2 if len(step) == 4 else 1
-                y = new("sum" + c, [P, M], F32)
+                pieces = 4 if step[3] == "q" else 2
+                width = M // pieces
+                whole = new("sum" + c, [P, M], F32) if "sum" + c in PLACES else None
                 for k in range(pieces):
-                    cols = slice(k * M // pieces, (k + 1) * M // pieces)
-                    adder = nc.gpsimd if step[:3] + "ab"[k] in ON_GPSIMD else nc.vector
-                    adder.tensor_tensor(out=y[:, cols], in0=t["mu" + c][:, cols], in1=placed[int(c)][:, cols], op=ADD)
-                    nc.sync.dma_start(out=out[int(c) * P : (int(c) + 1) * P, cols], in_=y[:, cols])
+                    cols = slice(k * width, (k + 1) * width)
+                    y = whole[:, cols] if whole is not None else new("sum" + c + "abcd"[k], [P, width], F32)[:]
+                    adder = nc.gpsimd if step[:3] + "abcd"[k] in ON_GPSIMD else nc.vector
+                    adder.tensor_tensor(out=y, in0=t["mu" + c][:, cols], in1=placed[int(c)][:, cols], op=ADD)
+                    nc.sync.dma_start(out=out[int(c) * P : (int(c) + 1) * P, cols], in_=y)
             elif step == "probe1":
                 probe(step, w_grouped[:, Q - 1 : Q, 0])
             elif step == "probe2":

from contextlib import ExitStack

import concourse.mybir as mybir
from concourse.masks import make_identity

D, T, I, Q, E, Z, M = 512, 2048, 512, 256, 512, 1024, 1024
FLOPS = 2 * D * Q * I + 2 * D * Q * Z + 2 * I * E * Q

F32 = mybir.dt.float32
BF16 = mybir.dt.bfloat16
I32 = mybir.dt.int32
U32 = mybir.dt.uint32
U16 = mybir.dt.uint16
U8 = mybir.dt.uint8
FP8X4 = mybir.dt.float8_e4m3fn_x4
COPY = mybir.ActivationFunctionType.Copy
MAX = mybir.AluOpType.max
MULT = mybir.AluOpType.mult
ADD = mybir.AluOpType.add

P = 128
PACK = 4
BANK = 512
Q_TILES = Q // P
E_TILES = E // P
Z_HALVES = Z // BANK
FADE_RUN = M // P
LOADS = ["q2","l1","fade","kb","p0","p1","q","kw","l2","v0","slot","v1","l3","v2","o0","v3","o1","o2","o3"]
STEPS = ["ilq2","gkb","qzq2","fade","ip0","qp0","ip1","qp1","ch00","ch01","ch10","ch11","ilq","qzq","gkw","gh0","gh1","gv0","mx0","mx1","mw0","mw1","cv0","gv1","qzw","qv0","gv2","cv1","co0","mu0","qv1","sc0","cv2","co1","gv3","qv2","sc1","cv3","mu1","co2","ad0h","qv3","sc2","mu2","co3","sc3","mu3","ad1h","ad2h","ad3q"]
ON_SCALAR = ["ips","ch00","ch01","ch10","ch11","gh0","gv0","gv1","cv0","cv1","cv2","cv3","co0","co1","co2","co3","sc0","sc1","sc2","sc3"]
PLACES = {"vals3":0,"vals2_codes":0,"old0":8192,"vals1_codes":8192,"old1":12288,"vals3_codes":12288,"sum0b":14336,"picked_vals1":16384,"result0":16384,"picked_vals2":17408,"result1":17408,"picked_vals3":18432,"result2":18432,"vals_grouped2":19456,"sum0a":19456,"sum1":21504,"vals_grouped3":25088,"faded2":25600,"sum3":25600,"old2":31744,"faded3":31744,"old3":35840,"sum2":35840,"pages_grouped1":44032,"q_grouped":44032,"picked_words":44032}
BANKS = {"ch00":0,"ch01":1,"ch10":2,"ch11":3,"mx1":5,"mx0":4,"mw1":1,"mw0":0,"f0":6,"f1":7,"cv0":5,"cv1":4,"cv2":5,"cv3":4,"co0":2,"co1":3,"co2":0,"co3":1}
PAGES_ON_VECTOR = 320
ON_GPSIMD = ["ad0a","ad1a","ad1b"]


def tile_attend_widelarger_written_lean_kernel(
    tc, query, query2, keys_words, keys_scales, pages, slot_scale, vals, old, fade, offs, offs2, offs3, out
):
    nc = tc.nc

    with ExitStack() as ctx:
        sb = ctx.enter_context(tc.tile_pool(name="sb", bufs=1))
        shared = ctx.enter_context(tc.tile_pool(name="shared", bufs=1))
        ps = ctx.enter_context(tc.psum_pool(name="ps", bufs=1))

        def bank(name, shape):
            return ps.tile(shape, F32, name=name, tag="bank%d" % BANKS[name])

        def new(name, shape, dtype, align=32):
            if name in PLACES:
                return shared.tile(shape, dtype, name=name, offset=PLACES[name], align_bytes=64)
            return sb.tile(shape, dtype, name=name, align_bytes=64)

        def load_rows(name, rows):
            raw = new(name, [P, PACK, rows.shape[1]], F32)
            nc.sync.dma_start(out=raw[:], in_=rows.rearrange("(p j) w -> p j w", j=PACK))
            return raw

        def load_plain(name, src, dtype):
            t = new(name, [P, src.shape[1]], dtype)
            nc.sync.dma_start(out=t[:], in_=src)
            return t

        def copy_on(step, dst, src):
            if step in ON_SCALAR:
                nc.scalar.copy(out=dst, in_=src)
            else:
                nc.vector.tensor_copy(out=dst, in_=src)

        def interleave(step, grouped, raw, cols):
            dst = grouped[:, cols, :].rearrange("p (c i) j -> p c j i", i=4)
            src = raw[:, :, cols].rearrange("p j (c i) -> p c j i", i=4)
            copy_on(step, dst, src)

        def quantise(name, grouped):
            width = grouped.shape[1]
            codes = new(name + "_codes", [P, width], U32)
            scales = new(name + "_scales", [P, width], U8)
            nc.vector.quantize_mx(
                out=codes[:].bitcast(FP8X4), scales=scales[:], in_=grouped[:].rearrange("p w j -> p (w j)")
            )
            return codes, scales

        def product(acc, stat, stat_cols, mov):
            nc.tensor.matmul_mx(
                out=acc,
                lhsT=stat[0][:, stat_cols].bitcast(FP8X4),
                lhsT_scale=stat[1][:, stat_cols],
                rhs=mov[0][:].bitcast(FP8X4),
                rhs_scale=mov[1][:],
                start=True,
                stop=True,
            )

        def listed(step, dst, src):
            if step in ON_SCALAR:
                nc.scalar.activation(out=dst, in_=src, func=COPY)
            else:
                nc.vector.tensor_copy(out=dst, in_=src)

        def probe(name, src):
            t = new(name, [P, src.shape[1]], src.dtype)
            nc.gpsimd.tensor_copy(out=t[:], in_=src)

        key_bytes = new("key_bytes", [P, T], U8)
        nc.gpsimd.memset(key_bytes[:].bitcast(I32), 0)
        placed = []
        for c in range(E_TILES):
            window = new("placed%d" % c, [P, M], F32)
            nc.vector.memset(window[:], 0.0)
            placed.append(window)
        identity = new("identity", [P, P], F32)
        make_identity(nc, identity[:])

        t = {}
        for name in LOADS:
            if name == "q2":
                t[name] = load_rows("q2_raw", query2)
            elif name == "q":
                t[name] = load_rows("q_raw", query)
            elif name in ("p0", "p1"):
                h = int(name[1])
                t[name] = load_rows("pages_raw%d" % h, pages[:, h * BANK : (h + 1) * BANK])
            elif name == "fade":
                t[name] = new("fade_runs", [P, 2, 4], F32)
                nc.sync.dma_start(out=t[name][:], in_=fade.rearrange("o (h n c) -> n (o h) c", h=2, c=4))
            elif name == "slot":
                t[name] = load_plain("slot_factor", slot_scale.rearrange("o (p t) -> (o p) t", t=PACK), F32)
            elif name == "l1":
                t[name] = load_plain("token_list", offs, U16)
            elif name == "l2":
                t[name] = load_plain("page_list", offs2, U16)
            elif name == "l3":
                t[name] = load_plain("column_list", offs3, U16)
            elif name == "kb":
                for quad in range(4):
                    nc.sync.dma_start(
                        out=key_bytes[32 * quad : 32 * quad + 4, :].bitcast(I32),
                        in_=keys_scales[0, 4 * quad : 4 * quad + 4, :].bitcast(I32),
                    )
            elif name == "kw":
                t[name] = new("key_words", [P, T], U32)
                nc.sync.dma_start(
                    out=t[name][:].bitcast(I32), in_=keys_words[0].rearrange("p n t -> p (n t)").bitcast(I32)
                )
            elif name[0] == "v":
                c = int(name[1])
                t[name] = load_plain("vals%d" % c, vals[c * P : (c + 1) * P, :], F32)
            else:
                c = int(name[1])
                t[name] = load_plain("old%d" % c, old[c * P : (c + 1) * P, :], F32)

        fade_ps = []
        h0 = [new("h0_%d" % r, [P, Z], F32) for r in range(Q_TILES)]
        w_grouped = new("w_grouped", [P, Q, PACK], BF16)

        for step in STEPS:
            kind, c = step[:2], step[2:3]
            if step in ("ilq", "ilq2"):
                name = step[2:]
                t["g" + name] = new(name + "_grouped", [P, Q, PACK], BF16)
                interleave(step, t["g" + name], t[name], slice(0, Q))
            elif step in ("qzq", "qzq2"):
                t["m" + step[2:]] = quantise(step[2:], t["g" + step[2:]])
            elif step == "fade":
                for h in range(FADE_RUN // 4):
                    spread = bank("f%d" % h, [P, 4, P])
                    for j in range(4):
                        nc.tensor.transpose(spread[:, j, :], t["fade"][:, h, j : j + 1].to_broadcast([P, P]), identity[:])
                    fade_ps.append(spread)
            elif kind == "ip":
                t["gp" + c] = new("pages_grouped" + c, [P, BANK, PACK], BF16)
                interleave("ipv", t["gp" + c], t["p" + c], slice(0, PAGES_ON_VECTOR))
                interleave("ips", t["gp" + c], t["p" + c], slice(PAGES_ON_VECTOR, BANK))
            elif kind == "qp":
                t["mp" + c] = quantise("pages" + c, t["gp" + c])
            elif kind == "ch":
                h, r = int(step[2]), int(step[3])
                acc = bank(step, [P, BANK])
                product(acc[:], t["mq2"], slice(r * P, (r + 1) * P), t["mp" + c])
                copy_on(step, h0[r][:, h * BANK : (h + 1) * BANK], acc[:])
            elif kind == "gh":
                t[step] = new("page_score" + c, [P, I], F32)
                listed(step, t[step][:], h0[int(c)][:].indirect(t["l2"][:]))
            elif step == "gkb":
                t[step] = new("picked_bytes", [P, I], U8)
                listed(step, t[step][:], key_bytes[:].indirect(t["l1"][:]))
            elif step == "gkw":
                t[step] = new("picked_words", [P, I], U32)
                listed(step, t[step][:], t["kw"][:].indirect(t["l1"][:]))
            elif kind == "mx":
                r = int(c)
                acc = bank(step, [P, I])
                product(acc[:], t["mq"], slice(r * P, (r + 1) * P), (t["gkw"], t["gkb"]))
                t[step] = new("score" + c, [P, PACK, P], F32)
                nc.vector.tensor_tensor(
                    out=t[step][:].rearrange("q t (a i) -> q a t i", i=4),
                    in0=acc[:].rearrange("q (a i t) -> q a t i", i=4, t=PACK),
                    in1=t["gh" + c][:].rearrange("q (a i t) -> q a t i", i=4, t=PACK),
                    op=MAX,
                )
            elif kind == "mw":
                r = int(c)
                turned_w = bank(step, [P, PACK, P])
                for j in range(PACK):
                    nc.tensor.transpose(turned_w[:, j, :], t["mx" + c][:, j, :], identity[:])
                nc.vector.scalar_tensor_tensor(
                    out=w_grouped[:, r * P : (r + 1) * P, :],
                    in0=turned_w[:].rearrange("p t q -> p q t"),
                    scalar=0.0,
                    in1=t["slot"][:].unsqueeze(1).to_broadcast([P, P, PACK]),
                    op0=MAX,
                    op1=MULT,
                )
            elif step == "qzw":
                t["mw"] = quantise("w", w_grouped)
            elif kind == "gv":
                t[step] = new("picked_vals" + c, [P, I], BF16)
                listed(step, t[step][:], t["v" + c][:].indirect(t["l1"][:]))
            elif kind == "cv":
                pairs = t["gv" + c][:].bitcast(F32)
                turned = bank(step, [P, 2, P])
                for u in range(2):
                    nc.tensor.transpose(turned[:, u, :], pairs[:, u : I // 2 : 2], identity[:])
                t[step] = new("vals_grouped" + c, [P, P, PACK], BF16)
                copy_on(step, t[step][:].bitcast(F32), turned[:].rearrange("p u e -> p e u"))
            elif kind == "qv":
                t[step] = quantise("vals" + c, t["cv" + c])
            elif kind == "co":
                acc = bank(step, [P, Q])
                product(acc[:], t["qv" + c], slice(0, P), t["mw"])
                t[step] = new("result" + c, [P, Q], F32)
                copy_on(step, t[step][:], acc[:])
            elif kind == "sc":
                listed(step, placed[int(c)][:].indirect(t["l3"][:]), t["co" + c][:])
            elif kind == "mu":
                t[step] = new("faded" + c, [P, M], F32)
                for h in range(2):
                    cols = slice(h * BANK, (h + 1) * BANK)
                    nc.vector.tensor_tensor(
                        out=t[step][:, cols].rearrange("p (n c) -> p n c", c=4),
                        in0=t["o" + c][:, cols].rearrange("p (n c) -> p n c", c=4),
                        in1=fade_ps[h][:].rearrange("p c n -> p n c"),
                        op=MULT,
                    )
            elif kind == "ad":
                pieces = 4 if step[3] == "q" else 2
                width = M // pieces
                whole = new("sum" + c, [P, M], F32) if "sum" + c in PLACES else None
                for k in range(pieces):
                    cols = slice(k * width, (k + 1) * width)
                    y = whole[:, cols] if whole is not None else new("sum" + c + "abcd"[k], [P, width], F32)[:]
                    adder = nc.gpsimd if step[:3] + "abcd"[k] in ON_GPSIMD else nc.vector
                    adder.tensor_tensor(out=y, in0=t["mu" + c][:, cols], in1=placed[int(c)][:, cols], op=ADD)
                    nc.sync.dma_start(out=out[int(c) * P : (int(c) + 1) * P, cols], in_=y)
            elif step == "probe1":
                probe(step, w_grouped[:, Q - 1 : Q, 0])
            elif step == "probe2":
                probe(step, t["co3"][:, 0:1])
